import numpy as np
import ml_dtypes


def mxq(x, axis, fmt="e4m3"):
    dtype, down = {"e4m3": (ml_dtypes.float8_e4m3fn, 7), "e5m2": (ml_dtypes.float8_e5m2, 14)}[fmt]
    v = np.moveaxis(np.asarray(x, np.float32).astype(ml_dtypes.bfloat16).astype(np.float64), axis, -1)
    blocks = v.reshape(v.shape[:-1] + (-1, 32))
    amax = np.abs(blocks).max(-1, keepdims=True)
    byte = np.maximum(np.where(amax > 0, np.frexp(amax)[1] - 1 + 127, 0) - down, 1)
    scale = np.exp2(byte - 127.0)
    codes = (blocks / scale).astype(np.float32).astype(dtype).astype(np.float64)
    return np.moveaxis((codes * scale).reshape(v.shape), -1, axis)


WIDE = False


def mx_kscale(k):
    if not WIDE:
        return np.ones(k)
    levels = np.array([10, -10, 5, -5, 0])
    if k % 512:
        return np.exp2(np.random.permutation(np.resize(levels, k // 32))).repeat(32)
    a = np.empty((k // 512, 16))
    for p in range(k // 512):
        a[p, :8] = np.random.permutation(np.resize(levels, 8))
        for g in range(8):
            far = levels[np.abs(levels - a[p, g]) >= 10]
            a[p, g + 8] = far[np.random.randint(len(far))]
    return np.exp2(a.ravel()).repeat(32)


def f64(x):
    return np.asarray(x).astype(np.float64)


def striped(idx):
    return np.tile(np.asarray(idx).reshape(-1, 16).T, (8, 1)).astype(np.uint16)


def unstriped(offs):
    return offs[:16].T.reshape(-1).astype(np.int64)


E2M1 = np.array([0.0, 0.5, 1.0, 1.5, 2.0, 3.0, 4.0, 6.0, -0.0, -0.5, -1.0, -1.5, -2.0, -3.0, -4.0, -6.0])


def pack_weight(w, fmt):
    k, n = w.shape
    w = f64(np.asarray(w, np.float32).astype(ml_dtypes.bfloat16)).reshape(k // 32, 32, n)
    amax = np.abs(w).max(1)
    if fmt == "e4m3":
        byte = np.frexp(amax)[1] - 1 + 127 - 7
    else:
        mant, ex = np.frexp(amax / 6.0)
        byte = np.where(mant > 0.5, ex, ex - 1) + 127
    byte = np.clip(np.where(amax > 0, byte, 1), 1, 254)
    scaled = (w * np.exp2(127.0 - byte)[:, None, :]).reshape(k, n).astype(np.float32)
    by_word = np.ascontiguousarray(scaled.reshape(k // 512, 128, 4, n).transpose(0, 1, 3, 2))
    if fmt == "e4m3":
        words = by_word.astype(ml_dtypes.float8_e4m3fn).view(np.uint8)
    else:
        c = by_word.astype(ml_dtypes.float4_e2m1fn).view(np.uint8) & 0xF
        words = (c[..., 0::2] | (c[..., 1::2] << 4)).reshape(k // 512, 128, 2 * n)
    return np.ascontiguousarray(words), np.ascontiguousarray(byte.astype(np.uint8).reshape(k // 512, 16, n))


def unpack_weight(words, scales, fmt):
    g, _, n = scales.shape
    words = np.ascontiguousarray(words).reshape(g, 128, n, -1)
    if fmt == "e4m3":
        vals = words.view(ml_dtypes.float8_e4m3fn).astype(np.float64)
    else:
        nib = np.empty((g, 128, n, 4), np.uint8)
        nib[..., 0::2] = words & 0xF
        nib[..., 1::2] = words >> 4
        vals = E2M1[nib]
    vals = vals * np.repeat(np.exp2(scales.astype(np.float64) - 127.0), 8, axis=1)[..., None]
    return vals.transpose(0, 1, 3, 2).reshape(g * 512, n)


def sigmoid(v):
    return 1.0 / (1.0 + np.exp(-v))


def bf(x):
    return np.asarray(x, np.float32).astype(ml_dtypes.bfloat16)


def planes(Y):
    r, m = Y.shape
    b = f64(bf(Y)).reshape(r // 32, 32, m)
    amax = np.abs(b).max(1)
    byte = np.clip(np.where(amax > 0, np.frexp(amax)[1] - 1 + 127 - 7, 1), 1, 254)
    codes = (b * np.exp2(127.0 - byte)[:, None, :]).reshape(r, m).astype(np.float32).astype(ml_dtypes.float8_e4m3fn).view(np.uint8)
    words = codes.reshape(r // 512, 128, 4, m).transpose(0, 1, 3, 2)
    return np.ascontiguousarray(words), np.ascontiguousarray(byte.astype(np.uint8).reshape(r // 512, 16, m))


K, R, F, T, J, G = 512, 512, 512, 2048, 256, 64


def setup_inputs():
    n = np.random.standard_normal
    idx = np.random.permutation(T)[:J]
    fk = mx_kscale(K)
    fr = mx_kscale(R)
    tabp = pack_weight(n((K, T)) / fk[:, None], "e2m1")
    dtabp = pack_weight(n((K, T)) / fk[:, None], "e2m1")
    return {
        "tab_words": tabp[0],
        "tab_scales": tabp[1],
        "dtab_words": dtabp[0],
        "dtab_scales": dtabp[1],
        "w1": (n((K, R)) * 1 / np.sqrt(K) * fk[:, None]).astype(np.float32),
        "temper": (np.random.uniform(0.5, 2.0, (R, 1))).astype(np.float32),
        "rs": (np.random.uniform(0.5, 2.0, (R, 1)) * fr[:, None]).astype(np.float32),
        "wor": (n((R, F)) * 1 / np.sqrt(R) / fr[:, None]).astype(np.float32),
        "res": (n((F, G)) * 0.5).astype(np.float32),
        "offs": striped(idx),
    }


def reference(tab_words, tab_scales, dtab_words, dtab_scales, w1, temper, rs, wor, res, offs):
    idx = unstriped(offs)
    tabu = unpack_weight(tab_words, tab_scales, "e2m1")
    dtabu = unpack_weight(dtab_words, dtab_scales, "e2m1")
    w1q = mxq(f64(w1), 0, "e4m3")
    tabidxg = tabu[:, idx]
    a = w1q.T @ tabidxg
    dtabidxg = dtabu[:, idx]
    ta = w1q.T @ dtabidxg
    p = np.exp(a * f64(temper))
    z = p.reshape(R, G, J // G).sum(axis=2)
    s = np.log(z) / f64(temper)
    tp = ta * f64(temper) * p
    tz = tp.reshape(R, G, J // G).sum(axis=2)
    ts = tz / z / f64(temper)
    tu1 = ts * sigmoid(s) * (1.0 + s * (1.0 - sigmoid(s)))
    fo1 = tu1 * f64(rs)
    worq = mxq(f64(wor), 0, "e4m3")
    fo1q = mxq(fo1, 0, "e4m3")
    yo = worq.T @ fo1q
    y = yo + f64(res)
    words, scales = planes(y)
    return y, words, scales

@@ -1,0 +1,250 @@
+from contextlib import ExitStack
+
+import concourse.mybir as mybir
+
+K, R, F, T, J, G = 512, 512, 512, 2048, 256, 64
+FLOPS = 2 * (2 * K * R * J + R * F * G)
+
+F32 = mybir.dt.float32
+BF16 = mybir.dt.bfloat16
+I32 = mybir.dt.int32
+U32 = mybir.dt.uint32
+U16 = mybir.dt.uint16
+U8 = mybir.dt.uint8
+FP8X4 = mybir.dt.float8_e4m3fn_x4
+FP4X4 = mybir.dt.float4_e2m1fn_x4
+ALU = mybir.AluOpType
+ACT = mybir.ActivationFunctionType
+AXIS = mybir.AxisListType
+
+P = 128
+PACK = 4
+POOL = J // G
+HALF = P // 2
+
+
+def load_scale_rows(queue, plane, rows):
+    for q in range(4):
+        queue.dma_start(out=plane[32 * q : 32 * q + 4, :].bitcast(I32), in_=rows[0, 4 * q : 4 * q + 4, :].bitcast(I32))
+
+
+def tile_attend_tcsoftmaxpool_o_pl_kernel(
+    tc, tab_words, tab_scales, dtab_words, dtab_scales, w1, temper, rs, wor, res, offs, out_0, out_1, out_2
+):
+    nc = tc.nc
+    with ExitStack() as ctx:
+        sb = ctx.enter_context(tc.tile_pool(name="sb", bufs=1))
+        ps = ctx.enter_context(tc.psum_pool(name="ps", bufs=1))
+
+        def tile(name, shape, dtype):
+            return sb.tile(shape, dtype, name=name, align_bytes=64)
+
+        offsets = sb.tile([P, J // 16], U16, name="offsets")
+        nc.sync.dma_start(offsets[:], offs)
+        t_words = tile("t_words", [P, T], U16)
+        nc.sync.dma_start(out=t_words[:].bitcast(I32), in_=tab_words[0].bitcast(I32))
+        t_plane = tile("t_plane", [P, T], U8)
+        nc.gpsimd.memset(t_plane[:].bitcast(I32), 0)
+        load_scale_rows(nc.scalar, t_plane, tab_scales)
+        d_plane = tile("d_plane", [P, T], U8)
+        nc.vector.memset(d_plane[:].bitcast(I32), 0)
+
+        def load_half(name, w, c):
+            rows = w.rearrange("(p j) c -> p j c", j=PACK)
+            raw = tile(name + str(c), [P, PACK, PACK * HALF], F32)
+            nc.sync.dma_start(out=raw[:], in_=rows[:, :, c * PACK * HALF : (c + 1) * PACK * HALF])
+            return raw
+
+        w1_raw = [load_half("w1_raw", w1, c) for c in range(2)]
+        wor_raw = [load_half("wor_raw", wor, 0)]
+        load_scale_rows(nc.sync, d_plane, dtab_scales)
+        wor_raw.append(load_half("wor_raw", wor, 1))
+        d_words = tile("d_words", [P, T], U16)
+        nc.sync.dma_start(out=d_words[:].bitcast(I32), in_=dtab_words[0].bitcast(I32))
+        res_sb = tile("res_sb", [P, PACK, G], F32)
+        nc.sync.dma_start(out=res_sb[:], in_=res.rearrange("(p t) g -> p t g", t=PACK))
+        temper_sb = tile("temper_sb", [P, PACK], F32)
+        nc.gpsimd.dma_start(out=temper_sb[:], in_=temper.rearrange("(p t) o -> p (t o)", t=PACK))
+        rs_sb = tile("rs_sb", [P, PACK], F32)
+        nc.gpsimd.dma_start(out=rs_sb[:], in_=rs.rearrange("(p t) o -> p (t o)", t=PACK))
+
+        def gather(name, words, plane):
+            g_words = tile(name + "_words", [P, J], U16)
+            nc.vector.tensor_copy(g_words[:], words[:].indirect(offsets[:]))
+            g_plane = tile(name + "_plane", [P, J], U8)
+            nc.vector.tensor_copy(g_plane[:], plane[:].indirect(offsets[:]))
+            return g_words, g_plane
+
+        tg_words, tg_plane = gather("tg", t_words, t_plane)
+
+        w1_codes = tile("w1_codes", [P, PACK, P], U32)
+        w1_plane = tile("w1_plane", [P, PACK, P], U8)
+        for c in range(2):
+            dealt = tile("w1_dealt" + str(c), [P, PACK, HALF, PACK], BF16)
+            nc.vector.tensor_copy(
+                out=dealt[:].rearrange("p t m j -> p m j t"),
+                in_=w1_raw[c][:].rearrange("p j (m t) -> p m j t", t=PACK),
+            )
+            cols = slice(c * HALF, (c + 1) * HALF)
+            for t in range(PACK):
+                nc.vector.quantize_mx(
+                    out=w1_codes[:, t, cols].bitcast(FP8X4),
+                    scales=w1_plane[:, t, cols],
+                    in_=dealt[:, t].rearrange("p m j -> p (m j)"),
+                )
+
+        def first_product(name, g_words, g_plane):
+            banks = []
+            for h in range(2):
+                bank = ps.tile([P, 2, J], F32, name=name + str(h))
+                for u in range(2):
+                    nc.tensor.matmul_mx(
+                        out=bank[:, u, :],
+                        lhsT=w1_codes[:, 2 * h + u, :].bitcast(FP8X4),
+                        lhsT_scale=w1_plane[:, 2 * h + u, :],
+                        rhs=g_words[:].bitcast(FP4X4),
+                        rhs_scale=g_plane[:],
+                        start=True,
+                        stop=True,
+                    )
+                banks.append(bank)
+            return banks
+
+        a_banks = first_product("a", tg_words, tg_plane)
+
+        rs_quarter = tile("rs_quarter", [P, PACK], F32)
+        nc.scalar.activation(out=rs_quarter[:], in_=rs_sb[:], func=ACT.Copy, scale=-0.25)
+        inv_temper = tile("inv_temper", [P, PACK], F32)
+        nc.vector.reciprocal(inv_temper[:], temper_sb[:])
+
+        top = tile("top", [P, PACK, 1, G], F32)
+        for h in range(2):
+            nc.vector.tensor_reduce(
+                out=top[:, 2 * h : 2 * h + 2].rearrange("p u o g -> p (u o g)"),
+                in_=a_banks[h][:].rearrange("p u (g i) -> p (u g) i", i=POOL),
+                axis=AXIS.X,
+                op=ALU.max,
+            )
+        below = tile("below", [P, PACK, POOL, G], F32)
+        p_sb = tile("p_sb", [P, PACK, POOL, G], F32)
+        for h in range(2):
+            nc.vector.tensor_tensor(
+                out=below[:, 2 * h : 2 * h + 2],
+                in0=a_banks[h][:].rearrange("p u (g i) -> p u i g", i=POOL),
+                in1=top[:, 2 * h : 2 * h + 2].broadcast_to([P, 2, POOL, G]),
+                op=ALU.subtract,
+            )
+            for t in range(2 * h, 2 * h + 2):
+                nc.scalar.activation(
+                    out=p_sb[:, t].rearrange("p i g -> p (i g)"),
+                    in_=below[:, t].rearrange("p i g -> p (i g)"),
+                    func=ACT.Exp,
+                    scale=temper_sb[:, t : t + 1],
+                )
+
+        dg_words, dg_plane = gather("dg", d_words, d_plane)
+        ta_banks = first_product("ta", dg_words, dg_plane)
+
+        wor_dealt = tile("wor_dealt", [P, PACK, P, PACK], BF16)
+        piece = HALF // 2
+        for c in range(2):
+            for e in range(2):
+                m0 = c * HALF + e * piece
+                nc.scalar.copy(
+                    out=wor_dealt[:, :, m0 : m0 + piece, :].rearrange("p t m j -> p m j t"),
+                    in_=wor_raw[c][:, :, e * piece * PACK : (e + 1) * piece * PACK].rearrange("p j (m t) -> p m j t", t=PACK),
+                )
+
+        def add_halves(name, src, n):
+            dst = tile(name, [P, PACK, n // 2, G], F32)
+            nc.vector.tensor_tensor(out=dst[:], in0=src[:, :, : n // 2, :], in1=src[:, :, n // 2 :, :], op=ALU.add)
+            return dst
+
+        def flat(x):
+            return x[:].rearrange("p t o g -> p (t o g)")
+
+        tp = tile("tp", [P, PACK, POOL, G], F32)
+
+        def weigh(h):
+            nc.vector.tensor_tensor(
+                out=tp[:, 2 * h : 2 * h + 2],
+                in0=ta_banks[h][:].rearrange("p u (g i) -> p u i g", i=POOL),
+                in1=p_sb[:, 2 * h : 2 * h + 2],
+                op=ALU.mult,
+            )
+
+        z2 = add_halves("z2", p_sb, POOL)
+        weigh(0)
+        z = add_halves("z", z2, 2)
+        log_z = tile("log_z", [P, PACK, 1, G], F32)
+        nc.scalar.activation(out=flat(log_z), in_=flat(z), func=ACT.Ln)
+        weigh(1)
+        s = tile("s", [P, PACK, 1, G], F32)
+        for t in range(PACK):
+            nc.vector.scalar_tensor_tensor(
+                out=s[:, t, 0, :], in0=log_z[:, t, 0, :], scalar=inv_temper[:, t : t + 1], in1=top[:, t, 0, :],
+                op0=ALU.mult, op1=ALU.add,
+            )
+        inv_z = tile("inv_z", [P, PACK, 1, G], F32)
+        nc.scalar.activation(out=flat(inv_z), in_=flat(log_z), func=ACT.Exp, scale=-1.0)
+        th = tile("th", [P, PACK, 1, G], F32)
+        nc.scalar.activation(out=flat(th), in_=flat(s), func=ACT.Tanh, scale=0.5)
+        th1 = tile("th1", [P, PACK, 1, G], F32)
+        nc.scalar.activation(out=flat(th1), in_=flat(th), func=ACT.Identity, bias=1.0)
+        tz2 = add_halves("tz2", tp, POOL)
+        wor_codes = tile("wor_codes", [P, PACK, P], U32)
+        wor_plane = tile("wor_plane", [P, PACK, P], U8)
+        nc.vector.quantize_mx(
+            out=wor_codes[:].rearrange("p t m -> p (t m)").bitcast(FP8X4),
+            scales=wor_plane[:].rearrange("p t m -> p (t m)"),
+            in_=wor_dealt[:].rearrange("p t m j -> p (t m j)"),
+        )
+        tz = add_halves("tz", tz2, 2)
+        q = tile("q", [P, PACK, 1, G], F32)
+        for t in range(PACK):
+            nc.vector.scalar_tensor_tensor(
+                out=q[:, t, 0, :], in0=tz[:, t, 0, :], scalar=rs_quarter[:, t : t + 1], in1=inv_z[:, t, 0, :],
+                op0=ALU.mult, op1=ALU.mult,
+            )
+        n = tile("n", [P, PACK, 1, G], F32)
+        nc.vector.scalar_tensor_tensor(out=flat(n), in0=flat(th), scalar=-1.0, in1=flat(s), op0=ALU.add, op1=ALU.mult)
+        c2 = tile("c2", [P, PACK, 1, G], F32)
+        nc.vector.scalar_tensor_tensor(out=flat(c2), in0=flat(n), scalar=-2.0, in1=flat(q), op0=ALU.add, op1=ALU.mult)
+        fo = tile("fo", [P, G, PACK], BF16)
+        nc.vector.tensor_tensor(
+            out=fo[:].rearrange("p (c i) t -> p c t i", i=4),
+            in0=c2[:].rearrange("p t o (c i) -> p c (t o) i", i=4),
+            in1=th1[:].rearrange("p t o (c i) -> p c (t o) i", i=4),
+            op=ALU.mult,
+        )
+        fo_codes = tile("fo_codes", [P, G], U32)
+        fo_plane = tile("fo_plane", [P, G], U8)
+        nc.vector.quantize_mx(out=fo_codes[:].bitcast(FP8X4), scales=fo_plane[:], in_=fo[:].rearrange("p g t -> p (g t)"))
+
+        yo = ps.tile([P, PACK, G], F32, name="yo")
+        for t in range(PACK):
+            nc.tensor.matmul_mx(
+                out=yo[:, t, :],
+                lhsT=wor_codes[:, t, :].bitcast(FP8X4),
+                lhsT_scale=wor_plane[:, t, :],
+                rhs=fo_codes[:].bitcast(FP8X4),
+                rhs_scale=fo_plane[:],
+                start=True,
+                stop=True,
+            )
+        y16 = tile("y16", [P, G, PACK], BF16)
+        nc.vector.tensor_tensor(
+            out=y16[:], in0=yo[:].rearrange("p t g -> p g t"), in1=res_sb[:].rearrange("p t g -> p g t"), op=ALU.add
+        )
+        y = tile("y", [P, PACK, G], F32)
+        nc.vector.tensor_tensor(out=y[:], in0=yo[:], in1=res_sb[:], op=ALU.add)
+        nc.sync.dma_start(out=out_0.rearrange("(p t) g -> p t g", t=PACK), in_=y[:])
+        y_codes = tile("y_codes", [P, G], U32)
+        y_plane = tile("y_plane", [P, G], U8)
+        nc.vector.quantize_mx(out=y_codes[:].bitcast(FP8X4), scales=y_plane[:], in_=y16[:].rearrange("p g t -> p (g t)"))
+        nc.scalar.dma_start(out=out_1[0].rearrange("p g r -> p (g r)").bitcast(I32), in_=y_codes[:].bitcast(I32))
+        for qd in range(4):
+            queue = nc.sync if qd % 2 == 0 else nc.scalar
+            queue.dma_start(
+                out=out_2[0, 4 * qd : 4 * qd + 4, :].bitcast(I32), in_=y_plane[32 * qd : 32 * qd + 4, :].bitcast(I32)
+            )

@@ -1,3 +1,4 @@
+import math
 from contextlib import ExitStack
 
 import concourse.mybir as mybir
@@ -21,6 +22,7 @@ P = 128
 PACK = 4
 POOL = J // G
 HALF = P // 2
+VECTOR_SHARE = 40
 
 
 def load_scale_rows(queue, plane, rows):
@@ -36,55 +38,46 @@ def tile_attend_tcsoftmaxpool_o_pl_kernel(
         sb = ctx.enter_context(tc.tile_pool(name="sb", bufs=1))
         ps = ctx.enter_context(tc.psum_pool(name="ps", bufs=1))
 
-        def tile(name, shape, dtype):
-            return sb.tile(shape, dtype, name=name, align_bytes=64)
+        def tile(name, shape, dtype, tag=""):
+            return sb.tile(shape, dtype, name=name, tag=tag or name, align_bytes=64)
 
         offsets = sb.tile([P, J // 16], U16, name="offsets")
         nc.sync.dma_start(offsets[:], offs)
-        t_words = tile("t_words", [P, T], U16)
+        t_words = tile("t_words", [P, T], U16, "stage0")
         nc.sync.dma_start(out=t_words[:].bitcast(I32), in_=tab_words[0].bitcast(I32))
-        t_plane = tile("t_plane", [P, T], U8)
+        t_plane = tile("t_plane", [P, T], U8, "stage1")
         nc.gpsimd.memset(t_plane[:].bitcast(I32), 0)
         load_scale_rows(nc.scalar, t_plane, tab_scales)
-        d_plane = tile("d_plane", [P, T], U8)
-        nc.vector.memset(d_plane[:].bitcast(I32), 0)
 
-        def load_half(name, w, c):
+        def load_half(name, w, c, tag):
             rows = w.rearrange("(p j) c -> p j c", j=PACK)
-            raw = tile(name + str(c), [P, PACK, PACK * HALF], F32)
+            raw = tile(name + str(c), [P, PACK, PACK * HALF], F32, tag)
             nc.sync.dma_start(out=raw[:], in_=rows[:, :, c * PACK * HALF : (c + 1) * PACK * HALF])
             return raw
 
-        w1_raw = [load_half("w1_raw", w1, c) for c in range(2)]
-        wor_raw = [load_half("wor_raw", wor, 0)]
-        load_scale_rows(nc.sync, d_plane, dtab_scales)
-        wor_raw.append(load_half("wor_raw", wor, 1))
-        d_words = tile("d_words", [P, T], U16)
-        nc.sync.dma_start(out=d_words[:].bitcast(I32), in_=dtab_words[0].bitcast(I32))
-        res_sb = tile("res_sb", [P, PACK, G], F32)
-        nc.sync.dma_start(out=res_sb[:], in_=res.rearrange("(p t) g -> p t g", t=PACK))
-        temper_sb = tile("temper_sb", [P, PACK], F32)
-        nc.gpsimd.dma_start(out=temper_sb[:], in_=temper.rearrange("(p t) o -> p (t o)", t=PACK))
-        rs_sb = tile("rs_sb", [P, PACK], F32)
-        nc.gpsimd.dma_start(out=rs_sb[:], in_=rs.rearrange("(p t) o -> p (t o)", t=PACK))
+        w1_raw = [load_half("w1_raw", w1, c, "stage" + str(2 + c)) for c in range(2)]
 
-        def gather(name, words, plane):
-            g_words = tile(name + "_words", [P, J], U16)
-            nc.vector.tensor_copy(g_words[:], words[:].indirect(offsets[:]))
-            g_plane = tile(name + "_plane", [P, J], U8)
-            nc.vector.tensor_copy(g_plane[:], plane[:].indirect(offsets[:]))
-            return g_words, g_plane
+        d_plane = tile("d_plane", [P, T], U8)
+        nc.vector.memset(d_plane[:].bitcast(I32), 0)
+        load_scale_rows(nc.gpsimd, d_plane, dtab_scales)
 
-        tg_words, tg_plane = gather("tg", t_words, t_plane)
+        def gather(name, window, dtype, tag):
+            listed = tile(name, [P, J], dtype, tag)
+            nc.vector.tensor_copy(listed[:], window[:].indirect(offsets[:]))
+            return listed
+
+        tg_words = gather("tg_words", t_words, U16, "listed_words")
+        tg_plane = gather("tg_plane", t_plane, U8, "listed_plane")
+        wor_raw = [load_half("wor_raw", wor, c, "stage" + str(c)) for c in range(2)]
 
         w1_codes = tile("w1_codes", [P, PACK, P], U32)
         w1_plane = tile("w1_plane", [P, PACK, P], U8)
         for c in range(2):
             dealt = tile("w1_dealt" + str(c), [P, PACK, HALF, PACK], BF16)
-            nc.vector.tensor_copy(
-                out=dealt[:].rearrange("p t m j -> p m j t"),
-                in_=w1_raw[c][:].rearrange("p j (m t) -> p m j t", t=PACK),
-            )
+            dst = dealt[:].rearrange("p t m j -> p m j t")
+            src = w1_raw[c][:].rearrange("p j (m t) -> p m j t", t=PACK)
+            nc.vector.tensor_copy(out=dst[:, :VECTOR_SHARE], in_=src[:, :VECTOR_SHARE])
+            nc.scalar.copy(out=dst[:, VECTOR_SHARE:], in_=src[:, VECTOR_SHARE:])
             cols = slice(c * HALF, (c + 1) * HALF)
             for t in range(PACK):
                 nc.vector.quantize_mx(
@@ -92,6 +85,11 @@ def tile_attend_tcsoftmaxpool_o_pl_kernel(
                     scales=w1_plane[:, t, cols],
                     in_=dealt[:, t].rearrange("p m j -> p (m j)"),
                 )
+
+        temper_sb = tile("temper_sb", [P, PACK], F32, "w1_dealt0")
+        nc.scalar.dma_start(out=temper_sb[:], in_=temper.rearrange("(p t) o -> p (t o)", t=PACK))
+        d_words = tile("d_words", [P, T], U16, "stage2")
+        nc.sync.dma_start(out=d_words[:].bitcast(I32), in_=dtab_words[0].bitcast(I32))
 
         def first_product(name, g_words, g_plane):
             banks = []
@@ -112,8 +110,6 @@ def tile_attend_tcsoftmaxpool_o_pl_kernel(
 
         a_banks = first_product("a", tg_words, tg_plane)
 
-        rs_quarter = tile("rs_quarter", [P, PACK], F32)
-        nc.scalar.activation(out=rs_quarter[:], in_=rs_sb[:], func=ACT.Copy, scale=-0.25)
         inv_temper = tile("inv_temper", [P, PACK], F32)
         nc.vector.reciprocal(inv_temper[:], temper_sb[:])
 
@@ -125,11 +121,11 @@ def tile_attend_tcsoftmaxpool_o_pl_kernel(
                 axis=AXIS.X,
                 op=ALU.max,
             )
-        below = tile("below", [P, PACK, POOL, G], F32)
         p_sb = tile("p_sb", [P, PACK, POOL, G], F32)
         for h in range(2):
+            below = tile("below" + str(h), [P, 2, POOL, G], F32)
             nc.vector.tensor_tensor(
-                out=below[:, 2 * h : 2 * h + 2],
+                out=below[:],
                 in0=a_banks[h][:].rearrange("p u (g i) -> p u i g", i=POOL),
                 in1=top[:, 2 * h : 2 * h + 2].broadcast_to([P, 2, POOL, G]),
                 op=ALU.subtract,
@@ -137,13 +133,11 @@ def tile_attend_tcsoftmaxpool_o_pl_kernel(
             for t in range(2 * h, 2 * h + 2):
                 nc.scalar.activation(
                     out=p_sb[:, t].rearrange("p i g -> p (i g)"),
-                    in_=below[:, t].rearrange("p i g -> p (i g)"),
+                    in_=below[:, t - 2 * h].rearrange("p i g -> p (i g)"),
                     func=ACT.Exp,
                     scale=temper_sb[:, t : t + 1],
                 )
 
-        dg_words, dg_plane = gather("dg", d_words, d_plane)
-        ta_banks = first_product("ta", dg_words, dg_plane)
 
         wor_dealt = tile("wor_dealt", [P, PACK, P, PACK], BF16)
         piece = HALF // 2
@@ -155,15 +149,19 @@ def tile_attend_tcsoftmaxpool_o_pl_kernel(
                     in_=wor_raw[c][:, :, e * piece * PACK : (e + 1) * piece * PACK].rearrange("p j (m t) -> p m j t", t=PACK),
                 )
 
-        def add_halves(name, src, n):
-            dst = tile(name, [P, PACK, n // 2, G], F32)
+        res_sb = tile("res_sb", [P, PACK, G], F32, "stage3")
+        nc.sync.dma_start(out=res_sb[:], in_=res.rearrange("(p t) g -> p t g", t=PACK))
+
+        rs_sb = tile("rs_sb", [P, PACK], F32, "w1_dealt1")
+        nc.sync.dma_start(out=rs_sb[:], in_=rs.rearrange("(p t) o -> p (t o)", t=PACK))
+
+        def add_halves(name, src, n, tag=""):
+            dst = tile(name, [P, PACK, n // 2, G], F32, tag)
             nc.vector.tensor_tensor(out=dst[:], in0=src[:, :, : n // 2, :], in1=src[:, :, n // 2 :, :], op=ALU.add)
             return dst
 
         def flat(x):
             return x[:].rearrange("p t o g -> p (t o g)")
-
-        tp = tile("tp", [P, PACK, POOL, G], F32)
 
         def weigh(h):
             nc.vector.tensor_tensor(
@@ -173,50 +171,58 @@ def tile_attend_tcsoftmaxpool_o_pl_kernel(
                 op=ALU.mult,
             )
 
+        dg_words = gather("dg_words", d_words, U16, "listed_words")
         z2 = add_halves("z2", p_sb, POOL)
-        weigh(0)
+        dg_plane = gather("dg_plane", d_plane, U8, "listed_plane")
+        ta_banks = first_product("ta", dg_words, dg_plane)
         z = add_halves("z", z2, 2)
+        tp = tile("tp", [P, PACK, POOL, G], F32, "z2")
         log_z = tile("log_z", [P, PACK, 1, G], F32)
         nc.scalar.activation(out=flat(log_z), in_=flat(z), func=ACT.Ln)
-        weigh(1)
+        weigh(0)
         s = tile("s", [P, PACK, 1, G], F32)
         for t in range(PACK):
             nc.vector.scalar_tensor_tensor(
                 out=s[:, t, 0, :], in0=log_z[:, t, 0, :], scalar=inv_temper[:, t : t + 1], in1=top[:, t, 0, :],
                 op0=ALU.mult, op1=ALU.add,
             )
+        weigh(1)
         inv_z = tile("inv_z", [P, PACK, 1, G], F32)
-        nc.scalar.activation(out=flat(inv_z), in_=flat(log_z), func=ACT.Exp, scale=-1.0)
+        nc.scalar.activation(out=flat(inv_z), in_=flat(log_z), func=ACT.Exp, scale=-1.0, bias=-math.log(4.0))
         th = tile("th", [P, PACK, 1, G], F32)
         nc.scalar.activation(out=flat(th), in_=flat(s), func=ACT.Tanh, scale=0.5)
-        th1 = tile("th1", [P, PACK, 1, G], F32)
-        nc.scalar.activation(out=flat(th1), in_=flat(th), func=ACT.Identity, bias=1.0)
         tz2 = add_halves("tz2", tp, POOL)
-        wor_codes = tile("wor_codes", [P, PACK, P], U32)
-        wor_plane = tile("wor_plane", [P, PACK, P], U8)
-        nc.vector.quantize_mx(
-            out=wor_codes[:].rearrange("p t m -> p (t m)").bitcast(FP8X4),
-            scales=wor_plane[:].rearrange("p t m -> p (t m)"),
-            in_=wor_dealt[:].rearrange("p t m j -> p (t m j)"),
+        tz = tile("tz", [P, PACK, G], F32)
+        nc.vector.scalar_tensor_tensor(
+            out=tz[:], in0=tz2[:, :, 0, :], scalar=-1.0, in1=tz2[:, :, 1, :], op0=ALU.mult, op1=ALU.subtract
         )
-        tz = add_halves("tz", tz2, 2)
+        n = tile("n", [P, PACK, 1, G], F32)
+        nc.vector.scalar_tensor_tensor(out=flat(n), in0=flat(th), scalar=-1.0, in1=flat(s), op0=ALU.add, op1=ALU.mult)
         q = tile("q", [P, PACK, 1, G], F32)
         for t in range(PACK):
             nc.vector.scalar_tensor_tensor(
-                out=q[:, t, 0, :], in0=tz[:, t, 0, :], scalar=rs_quarter[:, t : t + 1], in1=inv_z[:, t, 0, :],
+                out=q[:, t, 0, :], in0=tz[:, t, :], scalar=rs_sb[:, t : t + 1], in1=inv_z[:, t, 0, :],
                 op0=ALU.mult, op1=ALU.mult,
             )
-        n = tile("n", [P, PACK, 1, G], F32)
-        nc.vector.scalar_tensor_tensor(out=flat(n), in0=flat(th), scalar=-1.0, in1=flat(s), op0=ALU.add, op1=ALU.mult)
         c2 = tile("c2", [P, PACK, 1, G], F32)
-        nc.vector.scalar_tensor_tensor(out=flat(c2), in0=flat(n), scalar=-2.0, in1=flat(q), op0=ALU.add, op1=ALU.mult)
+        nc.vector.scalar_tensor_tensor(out=flat(c2), in0=flat(th), scalar=1.0, in1=flat(q), op0=ALU.add, op1=ALU.mult)
         fo = tile("fo", [P, G, PACK], BF16)
-        nc.vector.tensor_tensor(
-            out=fo[:].rearrange("p (c i) t -> p c t i", i=4),
-            in0=c2[:].rearrange("p t o (c i) -> p c (t o) i", i=4),
-            in1=th1[:].rearrange("p t o (c i) -> p c (t o) i", i=4),
-            op=ALU.mult,
+        nc.vector.scalar_tensor_tensor(
+            out=fo[:],
+            in0=n[:].rearrange("p t o g -> p g (t o)"),
+            scalar=-2.0,
+            in1=c2[:].rearrange("p t o g -> p g (t o)"),
+            op0=ALU.add,
+            op1=ALU.mult,
         )
+        wor_codes = tile("wor_codes", [P, PACK, P], U32)
+        wor_plane = tile("wor_plane", [P, PACK, P], U8)
+        for t in range(PACK):
+            nc.vector.quantize_mx(
+                out=wor_codes[:, t, :].bitcast(FP8X4),
+                scales=wor_plane[:, t, :],
+                in_=wor_dealt[:, t].rearrange("p m j -> p (m j)"),
+            )
         fo_codes = tile("fo_codes", [P, G], U32)
         fo_plane = tile("fo_plane", [P, G], U8)
         nc.vector.quantize_mx(out=fo_codes[:].bitcast(FP8X4), scales=fo_plane[:], in_=fo[:].rearrange("p g t -> p (g t)"))

import math
from contextlib import ExitStack

import concourse.mybir as mybir

K, R, F, T, J, G = 512, 512, 512, 2048, 256, 64
FLOPS = 2 * (2 * K * R * J + R * F * G)

F32 = mybir.dt.float32
BF16 = mybir.dt.bfloat16
I32 = mybir.dt.int32
U32 = mybir.dt.uint32
U16 = mybir.dt.uint16
U8 = mybir.dt.uint8
FP8X4 = mybir.dt.float8_e4m3fn_x4
FP4X4 = mybir.dt.float4_e2m1fn_x4
ALU = mybir.AluOpType
ACT = mybir.ActivationFunctionType
AXIS = mybir.AxisListType

P = 128
PACK = 4
POOL = J // G
HALF = P // 2
VECTOR_SHARE = 40


def load_scale_rows(queue, plane, rows):
    for q in range(4):
        queue.dma_start(out=plane[32 * q : 32 * q + 4, :].bitcast(I32), in_=rows[0, 4 * q : 4 * q + 4, :].bitcast(I32))


def tile_attend_tcsoftmaxpool_o_pl_kernel(
    tc, tab_words, tab_scales, dtab_words, dtab_scales, w1, temper, rs, wor, res, offs, out_0, out_1, out_2
):
    nc = tc.nc
    with ExitStack() as ctx:
        sb = ctx.enter_context(tc.tile_pool(name="sb", bufs=1))
        ps = ctx.enter_context(tc.psum_pool(name="ps", bufs=1))

        def tile(name, shape, dtype, tag=""):
            return sb.tile(shape, dtype, name=name, tag=tag or name, align_bytes=64)

        offsets = sb.tile([P, J // 16], U16, name="offsets")
        nc.sync.dma_start(offsets[:], offs)
        t_words = tile("t_words", [P, T], U16, "stage0")
        nc.sync.dma_start(out=t_words[:].bitcast(I32), in_=tab_words[0].bitcast(I32))
        t_plane = tile("t_plane", [P, T], U8, "stage1")
        nc.gpsimd.memset(t_plane[:].bitcast(I32), 0)
        load_scale_rows(nc.scalar, t_plane, tab_scales)

        def load_half(name, w, c, tag):
            rows = w.rearrange("(p j) c -> p j c", j=PACK)
            raw = tile(name + str(c), [P, PACK, PACK * HALF], F32, tag)
            nc.sync.dma_start(out=raw[:], in_=rows[:, :, c * PACK * HALF : (c + 1) * PACK * HALF])
            return raw

        w1_raw = [load_half("w1_raw", w1, c, "stage" + str(2 + c)) for c in range(2)]

        d_plane = tile("d_plane", [P, T], U8)
        nc.vector.memset(d_plane[:].bitcast(I32), 0)
        load_scale_rows(nc.gpsimd, d_plane, dtab_scales)

        def gather(name, window, dtype, tag):
            listed = tile(name, [P, J], dtype, tag)
            nc.vector.tensor_copy(listed[:], window[:].indirect(offsets[:]))
            return listed

        tg_words = gather("tg_words", t_words, U16, "listed_words")
        tg_plane = gather("tg_plane", t_plane, U8, "listed_plane")
        wor_raw = [load_half("wor_raw", wor, c, "stage" + str(c)) for c in range(2)]

        w1_codes = tile("w1_codes", [P, PACK, P], U32)
        w1_plane = tile("w1_plane", [P, PACK, P], U8)
        for c in range(2):
            dealt = tile("w1_dealt" + str(c), [P, PACK, HALF, PACK], BF16)
            dst = dealt[:].rearrange("p t m j -> p m j t")
            src = w1_raw[c][:].rearrange("p j (m t) -> p m j t", t=PACK)
            nc.vector.tensor_copy(out=dst[:, :VECTOR_SHARE], in_=src[:, :VECTOR_SHARE])
            nc.scalar.copy(out=dst[:, VECTOR_SHARE:], in_=src[:, VECTOR_SHARE:])
            cols = slice(c * HALF, (c + 1) * HALF)
            for t in range(PACK):
                nc.vector.quantize_mx(
                    out=w1_codes[:, t, cols].bitcast(FP8X4),
                    scales=w1_plane[:, t, cols],
                    in_=dealt[:, t].rearrange("p m j -> p (m j)"),
                )

        temper_sb = tile("temper_sb", [P, PACK], F32, "w1_dealt0")
        nc.scalar.dma_start(out=temper_sb[:], in_=temper.rearrange("(p t) o -> p (t o)", t=PACK))
        d_words = tile("d_words", [P, T], U16, "stage2")
        nc.sync.dma_start(out=d_words[:].bitcast(I32), in_=dtab_words[0].bitcast(I32))

        def first_product(name, g_words, g_plane):
            banks = []
            for h in range(2):
                bank = ps.tile([P, 2, J], F32, name=name + str(h))
                for u in range(2):
                    nc.tensor.matmul_mx(
                        out=bank[:, u, :],
                        lhsT=w1_codes[:, 2 * h + u, :].bitcast(FP8X4),
                        lhsT_scale=w1_plane[:, 2 * h + u, :],
                        rhs=g_words[:].bitcast(FP4X4),
                        rhs_scale=g_plane[:],
                        start=True,
                        stop=True,
                    )
                banks.append(bank)
            return banks

        a_banks = first_product("a", tg_words, tg_plane)

        inv_temper = tile("inv_temper", [P, PACK], F32)
        nc.vector.reciprocal(inv_temper[:], temper_sb[:])

        top = tile("top", [P, PACK, 1, G], F32)
        for h in range(2):
            nc.vector.tensor_reduce(
                out=top[:, 2 * h : 2 * h + 2].rearrange("p u o g -> p (u o g)"),
                in_=a_banks[h][:].rearrange("p u (g i) -> p (u g) i", i=POOL),
                axis=AXIS.X,
                op=ALU.max,
            )
        p_sb = tile("p_sb", [P, PACK, POOL, G], F32)
        for h in range(2):
            below = tile("below" + str(h), [P, 2, POOL, G], F32)
            nc.vector.tensor_tensor(
                out=below[:],
                in0=a_banks[h][:].rearrange("p u (g i) -> p u i g", i=POOL),
                in1=top[:, 2 * h : 2 * h + 2].broadcast_to([P, 2, POOL, G]),
                op=ALU.subtract,
            )
            for t in range(2 * h, 2 * h + 2):
                nc.scalar.activation(
                    out=p_sb[:, t].rearrange("p i g -> p (i g)"),
                    in_=below[:, t - 2 * h].rearrange("p i g -> p (i g)"),
                    func=ACT.Exp,
                    scale=temper_sb[:, t : t + 1],
                )


        wor_dealt = tile("wor_dealt", [P, PACK, P, PACK], BF16)
        piece = HALF // 2
        for c in range(2):
            for e in range(2):
                m0 = c * HALF + e * piece
                nc.scalar.copy(
                    out=wor_dealt[:, :, m0 : m0 + piece, :].rearrange("p t m j -> p m j t"),
                    in_=wor_raw[c][:, :, e * piece * PACK : (e + 1) * piece * PACK].rearrange("p j (m t) -> p m j t", t=PACK),
                )

        res_sb = tile("res_sb", [P, PACK, G], F32, "stage3")
        nc.sync.dma_start(out=res_sb[:], in_=res.rearrange("(p t) g -> p t g", t=PACK))

        rs_sb = tile("rs_sb", [P, PACK], F32, "w1_dealt1")
        nc.sync.dma_start(out=rs_sb[:], in_=rs.rearrange("(p t) o -> p (t o)", t=PACK))

        def add_halves(name, src, n, tag=""):
            dst = tile(name, [P, PACK, n // 2, G], F32, tag)
            nc.vector.tensor_tensor(out=dst[:], in0=src[:, :, : n // 2, :], in1=src[:, :, n // 2 :, :], op=ALU.add)
            return dst

        def flat(x):
            return x[:].rearrange("p t o g -> p (t o g)")

        def weigh(h):
            nc.vector.tensor_tensor(
                out=tp[:, 2 * h : 2 * h + 2],
                in0=ta_banks[h][:].rearrange("p u (g i) -> p u i g", i=POOL),
                in1=p_sb[:, 2 * h : 2 * h + 2],
                op=ALU.mult,
            )

        dg_words = gather("dg_words", d_words, U16, "listed_words")
        z2 = add_halves("z2", p_sb, POOL)
        dg_plane = gather("dg_plane", d_plane, U8, "listed_plane")
        ta_banks = first_product("ta", dg_words, dg_plane)
        z = add_halves("z", z2, 2)
        tp = tile("tp", [P, PACK, POOL, G], F32, "z2")
        log_z = tile("log_z", [P, PACK, 1, G], F32)
        nc.scalar.activation(out=flat(log_z), in_=flat(z), func=ACT.Ln)
        weigh(0)
        s = tile("s", [P, PACK, 1, G], F32)
        for t in range(PACK):
            nc.vector.scalar_tensor_tensor(
                out=s[:, t, 0, :], in0=log_z[:, t, 0, :], scalar=inv_temper[:, t : t + 1], in1=top[:, t, 0, :],
                op0=ALU.mult, op1=ALU.add,
            )
        weigh(1)
        inv_z = tile("inv_z", [P, PACK, 1, G], F32)
        nc.scalar.activation(out=flat(inv_z), in_=flat(log_z), func=ACT.Exp, scale=-1.0, bias=-math.log(4.0))
        th = tile("th", [P, PACK, 1, G], F32)
        nc.scalar.activation(out=flat(th), in_=flat(s), func=ACT.Tanh, scale=0.5)
        tz2 = add_halves("tz2", tp, POOL)
        tz = tile("tz", [P, PACK, G], F32)
        nc.vector.scalar_tensor_tensor(
            out=tz[:], in0=tz2[:, :, 0, :], scalar=-1.0, in1=tz2[:, :, 1, :], op0=ALU.mult, op1=ALU.subtract
        )
        n = tile("n", [P, PACK, 1, G], F32)
        nc.vector.scalar_tensor_tensor(out=flat(n), in0=flat(th), scalar=-1.0, in1=flat(s), op0=ALU.add, op1=ALU.mult)
        q = tile("q", [P, PACK, 1, G], F32)
        for t in range(PACK):
            nc.vector.scalar_tensor_tensor(
                out=q[:, t, 0, :], in0=tz[:, t, :], scalar=rs_sb[:, t : t + 1], in1=inv_z[:, t, 0, :],
                op0=ALU.mult, op1=ALU.mult,
            )
        c2 = tile("c2", [P, PACK, 1, G], F32)
        nc.vector.scalar_tensor_tensor(out=flat(c2), in0=flat(th), scalar=1.0, in1=flat(q), op0=ALU.add, op1=ALU.mult)
        fo = tile("fo", [P, G, PACK], BF16)
        nc.vector.scalar_tensor_tensor(
            out=fo[:],
            in0=n[:].rearrange("p t o g -> p g (t o)"),
            scalar=-2.0,
            in1=c2[:].rearrange("p t o g -> p g (t o)"),
            op0=ALU.add,
            op1=ALU.mult,
        )
        wor_codes = tile("wor_codes", [P, PACK, P], U32)
        wor_plane = tile("wor_plane", [P, PACK, P], U8)
        for t in range(PACK):
            nc.vector.quantize_mx(
                out=wor_codes[:, t, :].bitcast(FP8X4),
                scales=wor_plane[:, t, :],
                in_=wor_dealt[:, t].rearrange("p m j -> p (m j)"),
            )
        fo_codes = tile("fo_codes", [P, G], U32)
        fo_plane = tile("fo_plane", [P, G], U8)
        nc.vector.quantize_mx(out=fo_codes[:].bitcast(FP8X4), scales=fo_plane[:], in_=fo[:].rearrange("p g t -> p (g t)"))

        yo = ps.tile([P, PACK, G], F32, name="yo")
        for t in range(PACK):
            nc.tensor.matmul_mx(
                out=yo[:, t, :],
                lhsT=wor_codes[:, t, :].bitcast(FP8X4),
                lhsT_scale=wor_plane[:, t, :],
                rhs=fo_codes[:].bitcast(FP8X4),
                rhs_scale=fo_plane[:],
                start=True,
                stop=True,
            )
        y16 = tile("y16", [P, G, PACK], BF16)
        nc.vector.tensor_tensor(
            out=y16[:], in0=yo[:].rearrange("p t g -> p g t"), in1=res_sb[:].rearrange("p t g -> p g t"), op=ALU.add
        )
        y = tile("y", [P, PACK, G], F32)
        nc.vector.tensor_tensor(out=y[:], in0=yo[:], in1=res_sb[:], op=ALU.add)
        nc.sync.dma_start(out=out_0.rearrange("(p t) g -> p t g", t=PACK), in_=y[:])
        y_codes = tile("y_codes", [P, G], U32)
        y_plane = tile("y_plane", [P, G], U8)
        nc.vector.quantize_mx(out=y_codes[:].bitcast(FP8X4), scales=y_plane[:], in_=y16[:].rearrange("p g t -> p (g t)"))
        nc.scalar.dma_start(out=out_1[0].rearrange("p g r -> p (g r)").bitcast(I32), in_=y_codes[:].bitcast(I32))
        for qd in range(4):
            queue = nc.sync if qd % 2 == 0 else nc.scalar
            queue.dma_start(
                out=out_2[0, 4 * qd : 4 * qd + 4, :].bitcast(I32), in_=y_plane[32 * qd : 32 * qd + 4, :].bitcast(I32)
            )
